import numpy as np
import ml_dtypes


def mxq(x, axis, fmt="e4m3"):
    dtype, down = {"e4m3": (ml_dtypes.float8_e4m3fn, 7), "e5m2": (ml_dtypes.float8_e5m2, 14)}[fmt]
    v = np.moveaxis(np.asarray(x, np.float32).astype(ml_dtypes.bfloat16).astype(np.float64), axis, -1)
    blocks = v.reshape(v.shape[:-1] + (-1, 32))
    amax = np.abs(blocks).max(-1, keepdims=True)
    byte = np.maximum(np.where(amax > 0, np.frexp(amax)[1] - 1 + 127, 0) - down, 1)
    scale = np.exp2(byte - 127.0)
    codes = (blocks / scale).astype(np.float32).astype(dtype).astype(np.float64)
    return np.moveaxis((codes * scale).reshape(v.shape), -1, axis)


WIDE = False


def mx_kscale(k):
    if not WIDE:
        return np.ones(k)
    levels = np.array([10, -10, 5, -5, 0])
    if k % 512:
        return np.exp2(np.random.permutation(np.resize(levels, k // 32))).repeat(32)
    a = np.empty((k // 512, 16))
    for p in range(k // 512):
        a[p, :8] = np.random.permutation(np.resize(levels, 8))
        for g in range(8):
            far = levels[np.abs(levels - a[p, g]) >= 10]
            a[p, g + 8] = far[np.random.randint(len(far))]
    return np.exp2(a.ravel()).repeat(32)


def f64(x):
    return np.asarray(x).astype(np.float64)


def striped(idx):
    return np.tile(idx.reshape(-1, 16).T, (8, 1)).astype(np.uint16)


def unstriped(offs):
    return offs[:16].T.reshape(-1).astype(np.int64)


def striped8(idx):
    return np.concatenate([x.reshape(-1, 16).T for x in idx]).astype(np.uint16)


def runs(offs, k):
    lists = np.stack([offs[16 * r : 16 * r + 16].T.reshape(-1) for r in range(8)]).astype(np.int64)
    return lists[np.arange(k) % 512 // 64]


def pack_weight(w):
    k, n = w.shape
    w = f64(np.asarray(w, np.float32).astype(ml_dtypes.bfloat16)).reshape(k // 32, 32, n)
    amax = np.abs(w).max(1)
    byte = np.clip(np.where(amax > 0, np.frexp(amax)[1] - 1 + 127 - 7, 1), 1, 254)
    scaled = (w * np.exp2(127.0 - byte)[:, None, :]).reshape(k, n).astype(np.float32)
    words = np.ascontiguousarray(scaled.reshape(k // 512, 128, 4, n).transpose(0, 1, 3, 2)).astype(ml_dtypes.float8_e4m3fn).view(np.uint8)
    return words, np.ascontiguousarray(byte.astype(np.uint8).reshape(k // 512, 16, n))


def unpack_weight(words, scales):
    g, p, n, _ = words.shape
    vals = np.ascontiguousarray(words).view(ml_dtypes.float8_e4m3fn).astype(np.float64) * np.repeat(np.exp2(scales.astype(np.float64) - 127.0), 8, axis=1)[..., None]
    return vals.transpose(0, 1, 3, 2).reshape(g * 512, n)


def relu(v):
    return np.maximum(v, 0.0)

def planes(y):
    n, m = y.shape
    v = y.astype(np.float32).astype(ml_dtypes.bfloat16).astype(np.float64).reshape(n // 32, 32, m)
    top = np.abs(v).max(1)
    byte = np.clip(np.where(top > 0, np.frexp(top)[1] - 1 + 127 - 7, 1), 1, 254)
    codes = (v * np.exp2(127.0 - byte)[:, None, :]).reshape(n, m).astype(np.float32).astype(ml_dtypes.float8_e4m3fn).view(np.uint8)
    words = codes.reshape(n // 512, 128, 4, m).transpose(0, 1, 3, 2)
    return np.ascontiguousarray(words), np.ascontiguousarray(byte.astype(np.uint8).reshape(n // 512, 16, m))


K, T, S, N, H = 512, 2048, 512, 512, 512


def setup_inputs():
    n = np.random.standard_normal
    s = mx_kscale(K)[:, None]
    u = mx_kscale(H)
    packed_xT = pack_weight(n((K, T)) * s)
    packed_w1 = pack_weight(n((K, H)) / np.sqrt(K) / s)
    packed_w2 = pack_weight(n((H, N)) / np.sqrt(H) / u[:, None])
    return {
        "x_words": packed_xT[0],
        "x_scales": packed_xT[1],
        "w1_words": packed_w1[0],
        "w1_scales": packed_w1[1],
        "gn": (np.random.uniform(0.5, 1.5, (H, 1)) * u[:, None]).astype(np.float32),
        "w2_words": packed_w2[0],
        "w2_scales": packed_w2[1],
        "offs": striped(np.random.permutation(T)[:S]),
        "n1": striped8(np.stack([np.random.permutation(S) for _ in range(8)])),
        "n2": striped8(np.stack([np.random.permutation(S) for _ in range(8)])),
        "n3": striped8(np.stack([np.random.permutation(S) for _ in range(8)])),
    }


def reference(x_words, x_scales, w1_words, w1_scales, gn, w2_words, w2_scales, offs, n1, n2, n3):
    xq = unpack_weight(x_words, x_scales)[:, unstriped(offs)]
    y = unpack_weight(w1_words, w1_scales).T @ xq
    ex = np.exp(-1.0 * y)
    z = f64(gn) * (-1.0 * (np.log(ex + ex[np.arange(H)[:, None], runs(n1, H)])))
    h = unpack_weight(w2_words, w2_scales).T @ mxq(z, 0, "e4m3")
    out_0 = relu(np.maximum(h[np.arange(N)[:, None], runs(n2, N)], h[np.arange(N)[:, None], runs(n3, N)]) - h + 0.5)
    return (out_0,) + planes(out_0)

@@ -1,0 +1,204 @@
+from contextlib import ExitStack
+
+import concourse.mybir as mybir
+
+K, T, S, N, H = 512, 2048, 512, 512, 512
+FLOPS = 2 * K * H * S + 2 * H * N * S
+
+F32 = mybir.dt.float32
+BF16 = mybir.dt.bfloat16
+I32 = mybir.dt.int32
+U32 = mybir.dt.uint32
+U16 = mybir.dt.uint16
+U8 = mybir.dt.uint8
+FP8X4 = mybir.dt.float8_e4m3fn_x4
+ALU = mybir.AluOpType
+ACT = mybir.ActivationFunctionType
+
+P = 128
+PACK = 4
+HALF = S // 2
+STRIPE = 16
+OUT_CHUNKS = ((0, 256), (256, 384), (384, 512))
+
+
+def entries(lst, lo, hi):
+    return lst[:, lo // STRIPE : hi // STRIPE]
+
+
+def tile_picked_sminhinge_none_po_kernel(
+    tc, x_words, x_scales, w1_words, w1_scales, gn, w2_words, w2_scales, offs, n1, n2, n3, out_0, out_1, out_2
+):
+    nc = tc.nc
+    with ExitStack() as ctx:
+        keep = ctx.enter_context(tc.tile_pool(name="keep", bufs=1))
+        ring = ctx.enter_context(tc.tile_pool(name="ring", bufs=3))
+        psum = ctx.enter_context(tc.psum_pool(name="psum", bufs=1))
+
+        def words_view(ap):
+            return ap[0].rearrange("p c r -> p (c r)").bitcast(I32)
+
+        def load_scales_spread(dst, src, cols, quadrants):
+            rows = src[0].bitcast(I32)
+            for q in quadrants:
+                nc.sync.dma_start(
+                    out=dst[32 * q : 32 * q + 32, :].bitcast(I32),
+                    in_=rows[4 * q : 4 * q + 4, :].unsqueeze(0).to_broadcast([8, 4, cols // 4]),
+                )
+
+        offs_t = keep.tile([P, S // STRIPE], U16, name="offs_t")
+        n1_t = keep.tile([P, S // STRIPE], U16, name="n1_t")
+        n2_t = keep.tile([P, S // STRIPE], U16, name="n2_t")
+        n3_t = keep.tile([P, S // STRIPE], U16, name="n3_t")
+        xw = keep.tile([P, T], I32, name="xw", align_bytes=64)
+        xs = keep.tile([P, T], U8, name="xs", align_bytes=64)
+        w1w_raw = keep.tile([P, H], I32, name="w1w_raw")
+        w1s_raw = keep.tile([P, H], U8, name="w1s_raw")
+        w2w_raw = keep.tile([P, N], I32, name="w2w_raw")
+        w2s_raw = keep.tile([P, N], U8, name="w2s_raw")
+        gain = keep.tile([P, PACK], F32, name="gain")
+
+        nc.vector.memset(xs[:].bitcast(I32), 0)
+        nc.sync.dma_start(offs_t[:], offs)
+        load_scales_spread(w1s_raw, w1_scales, H, (0, 1))
+        nc.sync.dma_start(out=w1w_raw[:], in_=words_view(w1_words))
+        nc.sync.dma_start(out=xw[:], in_=words_view(x_words))
+        for q in range(4):
+            nc.scalar.dma_start(out=xs[32 * q : 32 * q + 4, :].bitcast(I32), in_=x_scales[0].bitcast(I32)[4 * q : 4 * q + 4, :])
+        load_scales_spread(w1s_raw, w1_scales, H, (2, 3))
+        nc.sync.dma_start(n1_t[:], n1)
+        nc.sync.dma_start(out=w2w_raw[:], in_=words_view(w2_words))
+        load_scales_spread(w2s_raw, w2_scales, N, range(4))
+        nc.sync.dma_start(out=gain[:], in_=gn.rearrange("(p t) o -> p (t o)", t=PACK))
+        nc.sync.dma_start(n2_t[:], n2)
+        nc.sync.dma_start(n3_t[:], n3)
+
+        def deal(raw, dtype, name):
+            dealt = keep.tile([P, raw.shape[1]], dtype, name=name, align_bytes=64)
+            nc.vector.tensor_copy(
+                out=dealt[:].rearrange("p (t m) -> p t m", t=PACK), in_=raw[:].rearrange("p (m t) -> p t m", t=PACK)
+            )
+            return dealt
+
+        gs = keep.tile([P, S], U8, name="gs", align_bytes=64)
+        nc.vector.tensor_copy(gs[:], xs[:].indirect(offs_t[:]))
+        w1w = deal(w1w_raw, I32, "w1w")
+        w1s = deal(w1s_raw, U8, "w1s")
+        gw = []
+        for h in range(2):
+            g = keep.tile([P, HALF], U32, name="gw%d" % h, align_bytes=64)
+            nc.vector.tensor_copy(g[:], xw[:].bitcast(U32).indirect(entries(offs_t, h * HALF, (h + 1) * HALF)))
+            gw.append(g)
+
+        def product(t, h, w_words, w_scales, codes, scales):
+            acc = psum.tile([P, HALF], F32, name="acc%d%d" % (t, h))
+            m = slice(t * P, (t + 1) * P)
+            nc.tensor.matmul_mx(
+                out=acc[:],
+                lhsT=w_words[:, m].bitcast(FP8X4),
+                lhsT_scale=w_scales[:, m],
+                rhs=codes.bitcast(FP8X4),
+                rhs_scale=scales,
+                start=True,
+                stop=True,
+            )
+            return acc
+
+        ex = [keep.tile([P, S], F32, name="ex%d" % t) for t in range(PACK)]
+        ex_copy = [keep.tile([P, S], F32, name="ex_copy%d" % t) for t in range(PACK)]
+        for t in range(PACK):
+            for h in range(2):
+                cols = slice(h * HALF, (h + 1) * HALF)
+                acc = product(t, h, w1w, w1s, gw[h][:], gs[:, cols])
+                nc.scalar.activation(ex[t][:, cols], acc[:], ACT.Exp, scale=-1.0)
+
+        w2w = deal(w2w_raw, I32, "w2w")
+        w2s = deal(w2s_raw, U8, "w2s")
+
+        sums = [keep.tile([P, PACK, HALF], F32, name="sums%d" % h) for h in range(2)]
+        for h in range(2):
+            cols = slice(h * HALF, (h + 1) * HALF)
+            for t in range(PACK):
+                if h == 0:
+                    nc.vector.tensor_copy(ex_copy[t][:], ex[t][:])
+                nc.vector.tensor_tensor(
+                    sums[h][:, t, :], ex[t][:].indirect(entries(n1_t, h * HALF, (h + 1) * HALF)), ex_copy[t][:, cols], ALU.add
+                )
+
+        zw = keep.tile([P, S], U32, name="zw", align_bytes=64)
+        zs = keep.tile([P, S], U8, name="zs", align_bytes=64)
+        hwin = [keep.tile([P, S], F32, name="hwin%d" % t) for t in range(PACK)]
+        hless = [keep.tile([P, S], F32, name="hless%d" % t) for t in range(PACK)]
+        accs = {}
+        for h in range(2):
+            cols = slice(h * HALF, (h + 1) * HALF)
+            logs = keep.tile([P, HALF, PACK], F32, name="logs%d" % h)
+            nc.scalar.activation(
+                logs[:].rearrange("p (c i) t -> p c t i", i=4), sums[h][:].rearrange("p t (c i) -> p c t i", i=4), ACT.Ln
+            )
+            zb = keep.tile([P, HALF, PACK], BF16, name="zb%d" % h, align_bytes=64)
+            nc.vector.scalar_tensor_tensor(
+                zb[:], logs[:], -1.0, gain[:].unsqueeze(1).to_broadcast([P, HALF, PACK]), ALU.mult, ALU.mult
+            )
+            nc.vector.quantize_mx(out=zw[:, cols].bitcast(FP8X4), scales=zs[:, cols], in_=zb[:].rearrange("p j t -> p (j t)"))
+            for t in range(PACK):
+                accs[t, h] = product(t, h, w2w, w2s, zw[:, cols], zs[:, cols])
+        for t in range(PACK):
+            for h in range(2):
+                cols = slice(h * HALF, (h + 1) * HALF)
+                nc.scalar.copy(hwin[t][:, cols], accs[t, h][:])
+                nc.scalar.activation(hless[t][:, cols], accs[t, h][:], ACT.Copy, bias=-0.5)
+
+        ow = keep.tile([P, S], U32, name="ow", align_bytes=64)
+        osc = keep.tile([P, S], U8, name="osc", align_bytes=64)
+        out_rows = out_0.rearrange("(p t) j -> p t j", t=PACK)
+        out_words = words_view(out_1)
+        res = [keep.tile([P, PACK, hi - lo], F32, name="res%d" % lo) for lo, hi in OUT_CHUNKS]
+
+        def margins(c, t):
+            lo, hi = OUT_CHUNKS[c]
+            pair = []
+            for name, lst in (("d2", n2_t), ("d3", n3_t)):
+                dd = ring.tile([P, hi - lo], F32, name=name)
+                nc.vector.tensor_tensor(dd[:], hwin[t][:].indirect(entries(lst, lo, hi)), hless[t][:, lo:hi], ALU.subtract)
+                pair.append(dd)
+            return pair
+
+        def hinge(c, t, pair):
+            nc.vector.scalar_tensor_tensor(res[c][:, t, :], pair[0][:], 0.0, pair[1][:], ALU.max, ALU.max)
+
+        def hand_out(c):
+            lo, hi = OUT_CHUNKS[c]
+            nc.sync.dma_start(out=out_rows[:, :, lo:hi], in_=res[c][:])
+            ob = keep.tile([P, hi - lo, PACK], BF16, name="ob%d" % c, align_bytes=64)
+            dst = ob[:].rearrange("p (c i) t -> p c t i", i=4)
+            src = res[c][:].rearrange("p t (c i) -> p c t i", i=4)
+            if c == len(OUT_CHUNKS) - 1:
+                nc.vector.tensor_copy(dst, src)
+            else:
+                nc.scalar.copy(dst, src)
+            return ob
+
+        def quantise(c, ob):
+            lo, hi = OUT_CHUNKS[c]
+            nc.vector.quantize_mx(out=ow[:, lo:hi].bitcast(FP8X4), scales=osc[:, lo:hi], in_=ob[:].rearrange("p j t -> p (j t)"))
+            nc.sync.dma_start(out=out_words[:, lo:hi], in_=ow[:, lo:hi].bitcast(I32))
+
+        steps = [(c, t) for c in range(len(OUT_CHUNKS)) for t in range(PACK)]
+        pending = None
+        rounded = {}
+        for c, t in steps:
+            pair = margins(c, t)
+            if pending is not None:
+                hinge(*pending)
+                if pending[1] == PACK - 1:
+                    rounded[pending[0]] = hand_out(pending[0])
+            if t == PACK - 1 and c > 0:
+                quantise(c - 1, rounded[c - 1])
+            pending = (c, t, pair)
+        hinge(*pending)
+        last = len(OUT_CHUNKS) - 1
+        quantise(last, hand_out(last))
+        for q in range(4):
+            eng = nc.scalar if q % 2 else nc.sync
+            eng.dma_start(out=out_2[0].bitcast(I32)[4 * q : 4 * q + 4, :], in_=osc[32 * q : 32 * q + 4, :].bitcast(I32))

@@ -32,7 +32,6 @@ def tile_picked_sminhinge_none_po_kernel(
     nc = tc.nc
     with ExitStack() as ctx:
         keep = ctx.enter_context(tc.tile_pool(name="keep", bufs=1))
-        ring = ctx.enter_context(tc.tile_pool(name="ring", bufs=3))
         psum = ctx.enter_context(tc.psum_pool(name="psum", bufs=1))
 
         def words_view(ap):
@@ -57,44 +56,41 @@ def tile_picked_sminhinge_none_po_kernel(
         w2w_raw = keep.tile([P, N], I32, name="w2w_raw")
         w2s_raw = keep.tile([P, N], U8, name="w2s_raw")
         gain = keep.tile([P, PACK], F32, name="gain")
+        neg_gain = keep.tile([P, PACK], F32, name="neg_gain")
 
         nc.vector.memset(xs[:].bitcast(I32), 0)
         nc.sync.dma_start(offs_t[:], offs)
-        load_scales_spread(w1s_raw, w1_scales, H, (0, 1))
         nc.sync.dma_start(out=w1w_raw[:], in_=words_view(w1_words))
-        nc.sync.dma_start(out=xw[:], in_=words_view(x_words))
         for q in range(4):
-            nc.scalar.dma_start(out=xs[32 * q : 32 * q + 4, :].bitcast(I32), in_=x_scales[0].bitcast(I32)[4 * q : 4 * q + 4, :])
-        load_scales_spread(w1s_raw, w1_scales, H, (2, 3))
+            nc.sync.dma_start(out=xs[32 * q : 32 * q + 4, :].bitcast(I32), in_=x_scales[0].bitcast(I32)[4 * q : 4 * q + 4, :])
+        nc.sync.dma_start(out=xw[:], in_=words_view(x_words))
+        load_scales_spread(w1s_raw, w1_scales, H, range(4))
         nc.sync.dma_start(n1_t[:], n1)
+        nc.sync.dma_start(out=gain[:], in_=gn.rearrange("(p t) o -> p (t o)", t=PACK))
         nc.sync.dma_start(out=w2w_raw[:], in_=words_view(w2_words))
         load_scales_spread(w2s_raw, w2_scales, N, range(4))
-        nc.sync.dma_start(out=gain[:], in_=gn.rearrange("(p t) o -> p (t o)", t=PACK))
         nc.sync.dma_start(n2_t[:], n2)
         nc.sync.dma_start(n3_t[:], n3)
 
         def deal(raw, dtype, name):
             dealt = keep.tile([P, raw.shape[1]], dtype, name=name, align_bytes=64)
             nc.vector.tensor_copy(
-                out=dealt[:].rearrange("p (t m) -> p t m", t=PACK), in_=raw[:].rearrange("p (m t) -> p t m", t=PACK)
+                out=dealt[:].rearrange("p (t m) -> p m t", t=PACK), in_=raw[:].rearrange("p (m t) -> p m t", t=PACK)
             )
             return dealt
 
         gs = keep.tile([P, S], U8, name="gs", align_bytes=64)
-        nc.vector.tensor_copy(gs[:], xs[:].indirect(offs_t[:]))
         w1w = deal(w1w_raw, I32, "w1w")
+        nc.vector.tensor_copy(gs[:], xs[:].indirect(offs_t[:]))
+        gw = [keep.tile([P, HALF], U32, name="gw%d" % h, align_bytes=64) for h in range(2)]
+        nc.vector.tensor_copy(gw[0][:], xw[:].bitcast(U32).indirect(entries(offs_t, 0, HALF)))
         w1s = deal(w1s_raw, U8, "w1s")
-        gw = []
-        for h in range(2):
-            g = keep.tile([P, HALF], U32, name="gw%d" % h, align_bytes=64)
-            nc.vector.tensor_copy(g[:], xw[:].bitcast(U32).indirect(entries(offs_t, h * HALF, (h + 1) * HALF)))
-            gw.append(g)
+        nc.vector.tensor_copy(gw[1][:], xw[:].bitcast(U32).indirect(entries(offs_t, HALF, S)))
 
-        def product(t, h, w_words, w_scales, codes, scales):
-            acc = psum.tile([P, HALF], F32, name="acc%d%d" % (t, h))
+        def product(acc, t, w_words, w_scales, codes, scales):
             m = slice(t * P, (t + 1) * P)
             nc.tensor.matmul_mx(
-                out=acc[:],
+                out=acc,
                 lhsT=w_words[:, m].bitcast(FP8X4),
                 lhsT_scale=w_scales[:, m],
                 rhs=codes.bitcast(FP8X4),
@@ -102,52 +98,65 @@ def tile_picked_sminhinge_none_po_kernel(
                 start=True,
                 stop=True,
             )
-            return acc
 
         ex = [keep.tile([P, S], F32, name="ex%d" % t) for t in range(PACK)]
-        ex_copy = [keep.tile([P, S], F32, name="ex_copy%d" % t) for t in range(PACK)]
+        ex_copy = [[keep.tile([P, HALF], F32, name="ex_copy%d%d" % (t, h)) for h in range(2)] for t in range(PACK)]
         for t in range(PACK):
             for h in range(2):
                 cols = slice(h * HALF, (h + 1) * HALF)
-                acc = product(t, h, w1w, w1s, gw[h][:], gs[:, cols])
+                acc = psum.tile([P, HALF], F32, name="acc%d%d" % (t, h))
+                product(acc[:], t, w1w, w1s, gw[h][:], gs[:, cols])
                 nc.scalar.activation(ex[t][:, cols], acc[:], ACT.Exp, scale=-1.0)
+            nc.sync.dma_start(out=ex_copy[t][1][:], in_=ex[t][:, HALF:S])
 
         w2w = deal(w2w_raw, I32, "w2w")
         w2s = deal(w2s_raw, U8, "w2s")
+        nc.vector.tensor_scalar(neg_gain[:], gain[:], -1.0, None, ALU.mult)
 
-        sums = [keep.tile([P, PACK, HALF], F32, name="sums%d" % h) for h in range(2)]
-        for h in range(2):
-            cols = slice(h * HALF, (h + 1) * HALF)
+        sums = [keep.tile([P, PACK, hi - lo], F32, name="sums%d" % lo) for lo, hi in OUT_CHUNKS]
+        for c, (lo, hi) in enumerate(OUT_CHUNKS):
+            h = lo // HALF
             for t in range(PACK):
-                if h == 0:
-                    nc.vector.tensor_copy(ex_copy[t][:], ex[t][:])
+                if c == 0:
+                    nc.vector.tensor_copy(ex_copy[t][0][:], ex[t][:, 0:HALF])
                 nc.vector.tensor_tensor(
-                    sums[h][:, t, :], ex[t][:].indirect(entries(n1_t, h * HALF, (h + 1) * HALF)), ex_copy[t][:, cols], ALU.add
+                    sums[c][:, t, :], ex[t][:].indirect(entries(n1_t, lo, hi)), ex_copy[t][h][:, lo - h * HALF : hi - h * HALF], ALU.add
                 )
 
         zw = keep.tile([P, S], U32, name="zw", align_bytes=64)
         zs = keep.tile([P, S], U8, name="zs", align_bytes=64)
         hwin = [keep.tile([P, S], F32, name="hwin%d" % t) for t in range(PACK)]
         hless = [keep.tile([P, S], F32, name="hless%d" % t) for t in range(PACK)]
-        accs = {}
+        accs = {(t, h): psum.tile([P, HALF], F32, name="acc%d%d" % (t, h)) for t in range(PACK) for h in range(2)}
+        for c, (lo, hi) in enumerate(OUT_CHUNKS):
+            h = lo // HALF
+            w = hi - lo
+            zb = keep.tile([P, w, PACK], BF16, name="zb%d" % c, align_bytes=64)
+            if c == 0:
+                logs = keep.tile([P, PACK, w], F32, name="logs%d" % c)
+                zp = keep.tile([P, PACK, w], BF16, name="zp")
+                for t in range(PACK):
+                    nc.scalar.activation(logs[:, t, :], sums[c][:, t, :], ACT.Ln)
+                for t in range(PACK):
+                    nc.scalar.activation(zp[:, t, :], logs[:, t, :], ACT.Copy, scale=neg_gain[:, t : t + 1])
+                nc.scalar.copy(zb[:].rearrange("p (c i) t -> p c t i", i=4), zp[:].rearrange("p t (c i) -> p c t i", i=4))
+            else:
+                logs = keep.tile([P, w, PACK], F32, name="logs%d" % c)
+                nc.scalar.activation(
+                    logs[:].rearrange("p (c i) t -> p c t i", i=4), sums[c][:].rearrange("p t (c i) -> p c t i", i=4), ACT.Ln
+                )
+                nc.vector.tensor_tensor(zb[:], logs[:], neg_gain[:].unsqueeze(1).to_broadcast([P, w, PACK]), ALU.mult)
+            nc.vector.quantize_mx(out=zw[:, lo:hi].bitcast(FP8X4), scales=zs[:, lo:hi], in_=zb[:].rearrange("p j t -> p (j t)"))
+            for t in range(PACK):
+                product(accs[t, h][:, lo - h * HALF : hi - h * HALF], t, w2w, w2s, zw[:, lo:hi], zs[:, lo:hi])
         for h in range(2):
             cols = slice(h * HALF, (h + 1) * HALF)
-            logs = keep.tile([P, HALF, PACK], F32, name="logs%d" % h)
-            nc.scalar.activation(
-                logs[:].rearrange("p (c i) t -> p c t i", i=4), sums[h][:].rearrange("p t (c i) -> p c t i", i=4), ACT.Ln
-            )
-            zb = keep.tile([P, HALF, PACK], BF16, name="zb%d" % h, align_bytes=64)
-            nc.vector.scalar_tensor_tensor(
-                zb[:], logs[:], -1.0, gain[:].unsqueeze(1).to_broadcast([P, HALF, PACK]), ALU.mult, ALU.mult
-            )
-            nc.vector.quantize_mx(out=zw[:, cols].bitcast(FP8X4), scales=zs[:, cols], in_=zb[:].rearrange("p j t -> p (j t)"))
             for t in range(PACK):
-                accs[t, h] = product(t, h, w2w, w2s, zw[:, cols], zs[:, cols])
-        for t in range(PACK):
-            for h in range(2):
-                cols = slice(h * HALF, (h + 1) * HALF)
                 nc.scalar.copy(hwin[t][:, cols], accs[t, h][:])
-                nc.scalar.activation(hless[t][:, cols], accs[t, h][:], ACT.Copy, bias=-0.5)
+                if h == 0:
+                    nc.scalar.activation(hless[t][:, cols], accs[t, h][:], ACT.Copy, bias=-0.5)
+        for t in range(PACK):
+            nc.scalar.activation(hless[t][:, HALF:S], accs[t, 1][:], ACT.Copy, bias=-0.5)
 
         ow = keep.tile([P, S], U32, name="ow", align_bytes=64)
         osc = keep.tile([P, S], U8, name="osc", align_bytes=64)
@@ -155,17 +164,14 @@ def tile_picked_sminhinge_none_po_kernel(
         out_words = words_view(out_1)
         res = [keep.tile([P, PACK, hi - lo], F32, name="res%d" % lo) for lo, hi in OUT_CHUNKS]
 
-        def margins(c, t):
+        def margins(c, tiles):
             lo, hi = OUT_CHUNKS[c]
-            pair = []
-            for name, lst in (("d2", n2_t), ("d3", n3_t)):
-                dd = ring.tile([P, hi - lo], F32, name=name)
-                nc.vector.tensor_tensor(dd[:], hwin[t][:].indirect(entries(lst, lo, hi)), hless[t][:, lo:hi], ALU.subtract)
-                pair.append(dd)
-            return pair
+            for t in tiles:
+                for dd, lst in ((d2[c], n2_t), (d3[c], n3_t)):
+                    nc.vector.tensor_tensor(dd[:, t, :], hwin[t][:].indirect(entries(lst, lo, hi)), hless[t][:, lo:hi], ALU.subtract)
 
-        def hinge(c, t, pair):
-            nc.vector.scalar_tensor_tensor(res[c][:, t, :], pair[0][:], 0.0, pair[1][:], ALU.max, ALU.max)
+        def hinge(c):
+            nc.vector.scalar_tensor_tensor(res[c][:], d2[c][:], 0.0, d3[c][:], ALU.max, ALU.max)
 
         def hand_out(c):
             lo, hi = OUT_CHUNKS[c]
@@ -184,20 +190,19 @@ def tile_picked_sminhinge_none_po_kernel(
             nc.vector.quantize_mx(out=ow[:, lo:hi].bitcast(FP8X4), scales=osc[:, lo:hi], in_=ob[:].rearrange("p j t -> p (j t)"))
             nc.sync.dma_start(out=out_words[:, lo:hi], in_=ow[:, lo:hi].bitcast(I32))
 
-        steps = [(c, t) for c in range(len(OUT_CHUNKS)) for t in range(PACK)]
-        pending = None
+        d2 = [keep.tile([P, PACK, hi - lo], F32, name="d2_%d" % lo) for lo, hi in OUT_CHUNKS]
+        d3 = [keep.tile([P, PACK, hi - lo], F32, name="d3_%d" % lo) for lo, hi in OUT_CHUNKS]
         rounded = {}
-        for c, t in steps:
-            pair = margins(c, t)
-            if pending is not None:
-                hinge(*pending)
-                if pending[1] == PACK - 1:
-                    rounded[pending[0]] = hand_out(pending[0])
-            if t == PACK - 1 and c > 0:
-                quantise(c - 1, rounded[c - 1])
-            pending = (c, t, pair)
-        hinge(*pending)
         last = len(OUT_CHUNKS) - 1
+        for c in range(len(OUT_CHUNKS)):
+            margins(c, range(1))
+            if c > 0:
+                hinge(c - 1)
+                rounded[c - 1] = hand_out(c - 1)
+            margins(c, range(1, PACK))
+            if c > 0:
+                quantise(c - 1, rounded[c - 1])
+        hinge(last)
         quantise(last, hand_out(last))
         for q in range(4):
             eng = nc.scalar if q % 2 else nc.sync

@@ -17,13 +17,27 @@ ACT = mybir.ActivationFunctionType
 
 P = 128
 PACK = 4
+QUADRANTS = 4
 HALF = S // 2
 STRIPE = 16
-OUT_CHUNKS = ((0, 256), (256, 384), (384, 512))
+LINE = 4
+CHUNKS = ((0, 256), (256, 384), (384, 512))
 
 
-def entries(lst, lo, hi):
-    return lst[:, lo // STRIPE : hi // STRIPE]
+def entries(list_tile, lo, hi):
+    return list_tile[:, lo // STRIPE : hi // STRIPE]
+
+
+def words_view(packed):
+    return packed[0].rearrange("p c r -> p (c r)").bitcast(I32)
+
+
+def by_lines_packed(tile_ap):
+    return tile_ap.rearrange("p (c i) t -> p c t i", i=LINE)
+
+
+def by_lines_planar(tile_ap):
+    return tile_ap.rearrange("p t (c i) -> p c t i", i=LINE)
 
 
 def tile_picked_sminhinge_none_po_kernel(
@@ -34,15 +48,12 @@ def tile_picked_sminhinge_none_po_kernel(
         keep = ctx.enter_context(tc.tile_pool(name="keep", bufs=1))
         psum = ctx.enter_context(tc.psum_pool(name="psum", bufs=1))
 
-        def words_view(ap):
-            return ap[0].rearrange("p c r -> p (c r)").bitcast(I32)
-
-        def load_scales_spread(dst, src, cols, quadrants):
+        def load_weight_scales(dst, src, columns):
             rows = src[0].bitcast(I32)
-            for q in quadrants:
+            for q in range(QUADRANTS):
                 nc.sync.dma_start(
                     out=dst[32 * q : 32 * q + 32, :].bitcast(I32),
-                    in_=rows[4 * q : 4 * q + 4, :].unsqueeze(0).to_broadcast([8, 4, cols // 4]),
+                    in_=rows[4 * q : 4 * q + 4, :].unsqueeze(0).to_broadcast([8, 4, columns // 4]),
                 )
 
         offs_t = keep.tile([P, S // STRIPE], U16, name="offs_t")
@@ -61,14 +72,14 @@ def tile_picked_sminhinge_none_po_kernel(
         nc.vector.memset(xs[:].bitcast(I32), 0)
         nc.sync.dma_start(offs_t[:], offs)
         nc.sync.dma_start(out=w1w_raw[:], in_=words_view(w1_words))
-        for q in range(4):
+        for q in range(QUADRANTS):
             nc.sync.dma_start(out=xs[32 * q : 32 * q + 4, :].bitcast(I32), in_=x_scales[0].bitcast(I32)[4 * q : 4 * q + 4, :])
         nc.sync.dma_start(out=xw[:], in_=words_view(x_words))
-        load_scales_spread(w1s_raw, w1_scales, H, range(4))
+        load_weight_scales(w1s_raw, w1_scales, H)
         nc.sync.dma_start(n1_t[:], n1)
         nc.sync.dma_start(out=gain[:], in_=gn.rearrange("(p t) o -> p (t o)", t=PACK))
         nc.sync.dma_start(out=w2w_raw[:], in_=words_view(w2_words))
-        load_scales_spread(w2s_raw, w2_scales, N, range(4))
+        load_weight_scales(w2s_raw, w2_scales, N)
         nc.sync.dma_start(n2_t[:], n2)
         nc.sync.dma_start(n3_t[:], n3)
 
@@ -82,7 +93,7 @@ def tile_picked_sminhinge_none_po_kernel(
         gs = keep.tile([P, S], U8, name="gs", align_bytes=64)
         w1w = deal(w1w_raw, I32, "w1w")
         nc.vector.tensor_copy(gs[:], xs[:].indirect(offs_t[:]))
-        gw = [keep.tile([P, HALF], U32, name="gw%d" % h, align_bytes=64) for h in range(2)]
+        gw = [keep.tile([P, HALF], U32, name="gw%d" % half, align_bytes=64) for half in range(2)]
         nc.vector.tensor_copy(gw[0][:], xw[:].bitcast(U32).indirect(entries(offs_t, 0, HALF)))
         w1s = deal(w1s_raw, U8, "w1s")
         nc.vector.tensor_copy(gw[1][:], xw[:].bitcast(U32).indirect(entries(offs_t, HALF, S)))
@@ -100,110 +111,122 @@ def tile_picked_sminhinge_none_po_kernel(
             )
 
         ex = [keep.tile([P, S], F32, name="ex%d" % t) for t in range(PACK)]
-        ex_copy = [[keep.tile([P, HALF], F32, name="ex_copy%d%d" % (t, h)) for h in range(2)] for t in range(PACK)]
+        ex_copy = [[keep.tile([P, HALF], F32, name="ex_copy%d%d" % (t, half)) for half in range(2)] for t in range(PACK)]
         for t in range(PACK):
-            for h in range(2):
-                cols = slice(h * HALF, (h + 1) * HALF)
-                acc = psum.tile([P, HALF], F32, name="acc%d%d" % (t, h))
-                product(acc[:], t, w1w, w1s, gw[h][:], gs[:, cols])
-                nc.scalar.activation(ex[t][:, cols], acc[:], ACT.Exp, scale=-1.0)
+            for half in range(2):
+                cols = slice(half * HALF, (half + 1) * HALF)
+                y_acc = psum.tile([P, HALF], F32, name="acc%d%d" % (t, half))
+                product(y_acc[:], t, w1w, w1s, gw[half][:], gs[:, cols])
+                nc.scalar.activation(ex[t][:, cols], y_acc[:], ACT.Exp, scale=-1.0)
             nc.sync.dma_start(out=ex_copy[t][1][:], in_=ex[t][:, HALF:S])
 
         w2w = deal(w2w_raw, I32, "w2w")
         w2s = deal(w2s_raw, U8, "w2s")
         nc.vector.tensor_scalar(neg_gain[:], gain[:], -1.0, None, ALU.mult)
 
-        sums = [keep.tile([P, PACK, hi - lo], F32, name="sums%d" % lo) for lo, hi in OUT_CHUNKS]
-        for c, (lo, hi) in enumerate(OUT_CHUNKS):
-            h = lo // HALF
+        sums = [keep.tile([P, PACK, hi - lo], F32, name="sums%d" % lo) for lo, hi in CHUNKS]
+        for c, (lo, hi) in enumerate(CHUNKS):
+            half = lo // HALF
             for t in range(PACK):
                 if c == 0:
                     nc.vector.tensor_copy(ex_copy[t][0][:], ex[t][:, 0:HALF])
                 nc.vector.tensor_tensor(
-                    sums[c][:, t, :], ex[t][:].indirect(entries(n1_t, lo, hi)), ex_copy[t][h][:, lo - h * HALF : hi - h * HALF], ALU.add
+                    sums[c][:, t, :],
+                    ex[t][:].indirect(entries(n1_t, lo, hi)),
+                    ex_copy[t][half][:, lo - half * HALF : hi - half * HALF],
+                    ALU.add,
                 )
 
         zw = keep.tile([P, S], U32, name="zw", align_bytes=64)
         zs = keep.tile([P, S], U8, name="zs", align_bytes=64)
-        hwin = [keep.tile([P, S], F32, name="hwin%d" % t) for t in range(PACK)]
-        hless = [keep.tile([P, S], F32, name="hless%d" % t) for t in range(PACK)]
-        accs = {(t, h): psum.tile([P, HALF], F32, name="acc%d%d" % (t, h)) for t in range(PACK) for h in range(2)}
-        for c, (lo, hi) in enumerate(OUT_CHUNKS):
-            h = lo // HALF
-            w = hi - lo
-            zb = keep.tile([P, w, PACK], BF16, name="zb%d" % c, align_bytes=64)
+        h_rows = [keep.tile([P, S], F32, name="h_rows%d" % t) for t in range(PACK)]
+        h_less = [keep.tile([P, S], F32, name="h_less%d" % t) for t in range(PACK)]
+
+        pieces = [CHUNKS, ((0, HALF), (HALF, S)), ((0, S),), ((0, S),)]
+        banks = [("acc00", "acc01", "acc21"), ("acc10", "acc11"), ("acc20",), ("acc30",)]
+        h_accs = [
+            [psum.tile([P, hi - lo], F32, name=bank) for (lo, hi), bank in zip(pieces[t], banks[t])] for t in range(PACK)
+        ]
+
+        def h_columns(t, lo, hi):
+            for (start, end), h_acc in zip(pieces[t], h_accs[t]):
+                if start <= lo and hi <= end:
+                    return h_acc[:, lo - start : hi - start]
+
+        for c, (lo, hi) in enumerate(CHUNKS):
+            width = hi - lo
+            zb = keep.tile([P, width, PACK], BF16, name="zb%d" % c, align_bytes=64)
             if c == 0:
-                logs = keep.tile([P, PACK, w], F32, name="logs%d" % c)
-                zp = keep.tile([P, PACK, w], BF16, name="zp")
+                logs = keep.tile([P, PACK, width], F32, name="logs%d" % c)
+                z_planar = keep.tile([P, PACK, width], BF16, name="z_planar")
                 for t in range(PACK):
                     nc.scalar.activation(logs[:, t, :], sums[c][:, t, :], ACT.Ln)
                 for t in range(PACK):
-                    nc.scalar.activation(zp[:, t, :], logs[:, t, :], ACT.Copy, scale=neg_gain[:, t : t + 1])
-                nc.scalar.copy(zb[:].rearrange("p (c i) t -> p c t i", i=4), zp[:].rearrange("p t (c i) -> p c t i", i=4))
+                    nc.scalar.activation(z_planar[:, t, :], logs[:, t, :], ACT.Copy, scale=neg_gain[:, t : t + 1])
+                nc.scalar.copy(by_lines_packed(zb[:]), by_lines_planar(z_planar[:]))
             else:
-                logs = keep.tile([P, w, PACK], F32, name="logs%d" % c)
-                nc.scalar.activation(
-                    logs[:].rearrange("p (c i) t -> p c t i", i=4), sums[c][:].rearrange("p t (c i) -> p c t i", i=4), ACT.Ln
-                )
-                nc.vector.tensor_tensor(zb[:], logs[:], neg_gain[:].unsqueeze(1).to_broadcast([P, w, PACK]), ALU.mult)
+                logs = keep.tile([P, width, PACK], F32, name="logs%d" % c)
+                nc.scalar.activation(by_lines_packed(logs[:]), by_lines_planar(sums[c][:]), ACT.Ln)
+                nc.vector.tensor_tensor(zb[:], logs[:], neg_gain[:].unsqueeze(1).to_broadcast([P, width, PACK]), ALU.mult)
             nc.vector.quantize_mx(out=zw[:, lo:hi].bitcast(FP8X4), scales=zs[:, lo:hi], in_=zb[:].rearrange("p j t -> p (j t)"))
             for t in range(PACK):
-                product(accs[t, h][:, lo - h * HALF : hi - h * HALF], t, w2w, w2s, zw[:, lo:hi], zs[:, lo:hi])
-        for h in range(2):
-            cols = slice(h * HALF, (h + 1) * HALF)
-            for t in range(PACK):
-                nc.scalar.copy(hwin[t][:, cols], accs[t, h][:])
-                if h == 0:
-                    nc.scalar.activation(hless[t][:, cols], accs[t, h][:], ACT.Copy, bias=-0.5)
+                product(h_columns(t, lo, hi), t, w2w, w2s, zw[:, lo:hi], zs[:, lo:hi])
+
         for t in range(PACK):
-            nc.scalar.activation(hless[t][:, HALF:S], accs[t, 1][:], ACT.Copy, bias=-0.5)
+            for n, ((lo, hi), h_acc) in enumerate(zip(pieces[t], h_accs[t])):
+                nc.scalar.copy(h_rows[t][:, lo:hi], h_acc[:])
+                if n == 0:
+                    nc.scalar.activation(h_less[t][:, lo:hi], h_acc[:], ACT.Copy, bias=-0.5)
+        for t in range(PACK):
+            for (lo, hi), h_acc in zip(pieces[t][1:], h_accs[t][1:]):
+                nc.scalar.activation(h_less[t][:, lo:hi], h_acc[:], ACT.Copy, bias=-0.5)
 
         ow = keep.tile([P, S], U32, name="ow", align_bytes=64)
         osc = keep.tile([P, S], U8, name="osc", align_bytes=64)
         out_rows = out_0.rearrange("(p t) j -> p t j", t=PACK)
         out_words = words_view(out_1)
-        res = [keep.tile([P, PACK, hi - lo], F32, name="res%d" % lo) for lo, hi in OUT_CHUNKS]
+        res = [keep.tile([P, PACK, hi - lo], F32, name="res%d" % lo) for lo, hi in CHUNKS]
+        d2 = [keep.tile([P, PACK, hi - lo], F32, name="d2_%d" % lo) for lo, hi in CHUNKS]
+        d3 = [keep.tile([P, PACK, hi - lo], F32, name="d3_%d" % lo) for lo, hi in CHUNKS]
+        last = len(CHUNKS) - 1
 
         def margins(c, tiles):
-            lo, hi = OUT_CHUNKS[c]
+            lo, hi = CHUNKS[c]
             for t in tiles:
-                for dd, lst in ((d2[c], n2_t), (d3[c], n3_t)):
-                    nc.vector.tensor_tensor(dd[:, t, :], hwin[t][:].indirect(entries(lst, lo, hi)), hless[t][:, lo:hi], ALU.subtract)
+                for margin, list_tile in ((d2[c], n2_t), (d3[c], n3_t)):
+                    nc.vector.tensor_tensor(
+                        margin[:, t, :], h_rows[t][:].indirect(entries(list_tile, lo, hi)), h_less[t][:, lo:hi], ALU.subtract
+                    )
 
         def hinge(c):
             nc.vector.scalar_tensor_tensor(res[c][:], d2[c][:], 0.0, d3[c][:], ALU.max, ALU.max)
 
-        def hand_out(c):
-            lo, hi = OUT_CHUNKS[c]
+        def store_and_round(c):
+            lo, hi = CHUNKS[c]
             nc.sync.dma_start(out=out_rows[:, :, lo:hi], in_=res[c][:])
             ob = keep.tile([P, hi - lo, PACK], BF16, name="ob%d" % c, align_bytes=64)
-            dst = ob[:].rearrange("p (c i) t -> p c t i", i=4)
-            src = res[c][:].rearrange("p t (c i) -> p c t i", i=4)
-            if c == len(OUT_CHUNKS) - 1:
-                nc.vector.tensor_copy(dst, src)
+            if c == last:
+                nc.vector.tensor_copy(by_lines_packed(ob[:]), by_lines_planar(res[c][:]))
             else:
-                nc.scalar.copy(dst, src)
+                nc.scalar.copy(by_lines_packed(ob[:]), by_lines_planar(res[c][:]))
             return ob
 
         def quantise(c, ob):
-            lo, hi = OUT_CHUNKS[c]
+            lo, hi = CHUNKS[c]
             nc.vector.quantize_mx(out=ow[:, lo:hi].bitcast(FP8X4), scales=osc[:, lo:hi], in_=ob[:].rearrange("p j t -> p (j t)"))
             nc.sync.dma_start(out=out_words[:, lo:hi], in_=ow[:, lo:hi].bitcast(I32))
 
-        d2 = [keep.tile([P, PACK, hi - lo], F32, name="d2_%d" % lo) for lo, hi in OUT_CHUNKS]
-        d3 = [keep.tile([P, PACK, hi - lo], F32, name="d3_%d" % lo) for lo, hi in OUT_CHUNKS]
-        rounded = {}
-        last = len(OUT_CHUNKS) - 1
-        for c in range(len(OUT_CHUNKS)):
+        for c in range(len(CHUNKS)):
             margins(c, range(1))
             if c > 0:
                 hinge(c - 1)
-                rounded[c - 1] = hand_out(c - 1)
+                rounded = store_and_round(c - 1)
             margins(c, range(1, PACK))
             if c > 0:
-                quantise(c - 1, rounded[c - 1])
+                quantise(c - 1, rounded)
         hinge(last)
-        quantise(last, hand_out(last))
-        for q in range(4):
-            eng = nc.scalar if q % 2 else nc.sync
-            eng.dma_start(out=out_2[0].bitcast(I32)[4 * q : 4 * q + 4, :], in_=osc[32 * q : 32 * q + 4, :].bitcast(I32))
+        quantise(last, store_and_round(last))
+
+        for q in range(QUADRANTS):
+            queue = nc.scalar if q % 2 else nc.sync
+            queue.dma_start(out=out_2[0].bitcast(I32)[4 * q : 4 * q + 4, :], in_=osc[32 * q : 32 * q + 4, :].bitcast(I32))

from contextlib import ExitStack

import concourse.mybir as mybir

K, T, S, N, H = 512, 2048, 512, 512, 512
FLOPS = 2 * K * H * S + 2 * H * N * S

F32 = mybir.dt.float32
BF16 = mybir.dt.bfloat16
I32 = mybir.dt.int32
U32 = mybir.dt.uint32
U16 = mybir.dt.uint16
U8 = mybir.dt.uint8
FP8X4 = mybir.dt.float8_e4m3fn_x4
ALU = mybir.AluOpType
ACT = mybir.ActivationFunctionType

P = 128
PACK = 4
QUADRANTS = 4
HALF = S // 2
STRIPE = 16
LINE = 4
CHUNKS = ((0, 256), (256, 384), (384, 512))


def entries(list_tile, lo, hi):
    return list_tile[:, lo // STRIPE : hi // STRIPE]


def words_view(packed):
    return packed[0].rearrange("p c r -> p (c r)").bitcast(I32)


def by_lines_packed(tile_ap):
    return tile_ap.rearrange("p (c i) t -> p c t i", i=LINE)


def by_lines_planar(tile_ap):
    return tile_ap.rearrange("p t (c i) -> p c t i", i=LINE)


def tile_picked_sminhinge_none_po_kernel(
    tc, x_words, x_scales, w1_words, w1_scales, gn, w2_words, w2_scales, offs, n1, n2, n3, out_0, out_1, out_2
):
    nc = tc.nc
    with ExitStack() as ctx:
        keep = ctx.enter_context(tc.tile_pool(name="keep", bufs=1))
        psum = ctx.enter_context(tc.psum_pool(name="psum", bufs=1))

        def load_weight_scales(dst, src, columns):
            rows = src[0].bitcast(I32)
            for q in range(QUADRANTS):
                nc.sync.dma_start(
                    out=dst[32 * q : 32 * q + 32, :].bitcast(I32),
                    in_=rows[4 * q : 4 * q + 4, :].unsqueeze(0).to_broadcast([8, 4, columns // 4]),
                )

        offs_t = keep.tile([P, S // STRIPE], U16, name="offs_t")
        n1_t = keep.tile([P, S // STRIPE], U16, name="n1_t")
        n2_t = keep.tile([P, S // STRIPE], U16, name="n2_t")
        n3_t = keep.tile([P, S // STRIPE], U16, name="n3_t")
        xw = keep.tile([P, T], I32, name="xw", align_bytes=64)
        xs = keep.tile([P, T], U8, name="xs", align_bytes=64)
        w1w_raw = keep.tile([P, H], I32, name="w1w_raw")
        w1s_raw = keep.tile([P, H], U8, name="w1s_raw")
        w2w_raw = keep.tile([P, N], I32, name="w2w_raw")
        w2s_raw = keep.tile([P, N], U8, name="w2s_raw")
        gain = keep.tile([P, PACK], F32, name="gain")
        neg_gain = keep.tile([P, PACK], F32, name="neg_gain")

        nc.vector.memset(xs[:].bitcast(I32), 0)
        nc.sync.dma_start(offs_t[:], offs)
        nc.sync.dma_start(out=w1w_raw[:], in_=words_view(w1_words))
        for q in range(QUADRANTS):
            nc.sync.dma_start(out=xs[32 * q : 32 * q + 4, :].bitcast(I32), in_=x_scales[0].bitcast(I32)[4 * q : 4 * q + 4, :])
        nc.sync.dma_start(out=xw[:], in_=words_view(x_words))
        load_weight_scales(w1s_raw, w1_scales, H)
        nc.sync.dma_start(n1_t[:], n1)
        nc.sync.dma_start(out=gain[:], in_=gn.rearrange("(p t) o -> p (t o)", t=PACK))
        nc.sync.dma_start(out=w2w_raw[:], in_=words_view(w2_words))
        load_weight_scales(w2s_raw, w2_scales, N)
        nc.sync.dma_start(n2_t[:], n2)
        nc.sync.dma_start(n3_t[:], n3)

        def deal(raw, dtype, name):
            dealt = keep.tile([P, raw.shape[1]], dtype, name=name, align_bytes=64)
            nc.vector.tensor_copy(
                out=dealt[:].rearrange("p (t m) -> p m t", t=PACK), in_=raw[:].rearrange("p (m t) -> p m t", t=PACK)
            )
            return dealt

        gs = keep.tile([P, S], U8, name="gs", align_bytes=64)
        w1w = deal(w1w_raw, I32, "w1w")
        nc.vector.tensor_copy(gs[:], xs[:].indirect(offs_t[:]))
        gw = [keep.tile([P, HALF], U32, name="gw%d" % half, align_bytes=64) for half in range(2)]
        nc.vector.tensor_copy(gw[0][:], xw[:].bitcast(U32).indirect(entries(offs_t, 0, HALF)))
        w1s = deal(w1s_raw, U8, "w1s")
        nc.vector.tensor_copy(gw[1][:], xw[:].bitcast(U32).indirect(entries(offs_t, HALF, S)))

        def product(acc, t, w_words, w_scales, codes, scales):
            m = slice(t * P, (t + 1) * P)
            nc.tensor.matmul_mx(
                out=acc,
                lhsT=w_words[:, m].bitcast(FP8X4),
                lhsT_scale=w_scales[:, m],
                rhs=codes.bitcast(FP8X4),
                rhs_scale=scales,
                start=True,
                stop=True,
            )

        ex = [keep.tile([P, S], F32, name="ex%d" % t) for t in range(PACK)]
        ex_copy = [[keep.tile([P, HALF], F32, name="ex_copy%d%d" % (t, half)) for half in range(2)] for t in range(PACK)]
        for t in range(PACK):
            for half in range(2):
                cols = slice(half * HALF, (half + 1) * HALF)
                y_acc = psum.tile([P, HALF], F32, name="acc%d%d" % (t, half))
                product(y_acc[:], t, w1w, w1s, gw[half][:], gs[:, cols])
                nc.scalar.activation(ex[t][:, cols], y_acc[:], ACT.Exp, scale=-1.0)
            nc.sync.dma_start(out=ex_copy[t][1][:], in_=ex[t][:, HALF:S])

        w2w = deal(w2w_raw, I32, "w2w")
        w2s = deal(w2s_raw, U8, "w2s")
        nc.vector.tensor_scalar(neg_gain[:], gain[:], -1.0, None, ALU.mult)

        sums = [keep.tile([P, PACK, hi - lo], F32, name="sums%d" % lo) for lo, hi in CHUNKS]
        for c, (lo, hi) in enumerate(CHUNKS):
            half = lo // HALF
            for t in range(PACK):
                if c == 0:
                    nc.vector.tensor_copy(ex_copy[t][0][:], ex[t][:, 0:HALF])
                nc.vector.tensor_tensor(
                    sums[c][:, t, :],
                    ex[t][:].indirect(entries(n1_t, lo, hi)),
                    ex_copy[t][half][:, lo - half * HALF : hi - half * HALF],
                    ALU.add,
                )

        zw = keep.tile([P, S], U32, name="zw", align_bytes=64)
        zs = keep.tile([P, S], U8, name="zs", align_bytes=64)
        h_rows = [keep.tile([P, S], F32, name="h_rows%d" % t) for t in range(PACK)]
        h_less = [keep.tile([P, S], F32, name="h_less%d" % t) for t in range(PACK)]

        pieces = [CHUNKS, ((0, HALF), (HALF, S)), ((0, S),), ((0, S),)]
        banks = [("acc00", "acc01", "acc21"), ("acc10", "acc11"), ("acc20",), ("acc30",)]
        h_accs = [
            [psum.tile([P, hi - lo], F32, name=bank) for (lo, hi), bank in zip(pieces[t], banks[t])] for t in range(PACK)
        ]

        def h_columns(t, lo, hi):
            for (start, end), h_acc in zip(pieces[t], h_accs[t]):
                if start <= lo and hi <= end:
                    return h_acc[:, lo - start : hi - start]

        for c, (lo, hi) in enumerate(CHUNKS):
            width = hi - lo
            zb = keep.tile([P, width, PACK], BF16, name="zb%d" % c, align_bytes=64)
            if c == 0:
                logs = keep.tile([P, PACK, width], F32, name="logs%d" % c)
                z_planar = keep.tile([P, PACK, width], BF16, name="z_planar")
                for t in range(PACK):
                    nc.scalar.activation(logs[:, t, :], sums[c][:, t, :], ACT.Ln)
                for t in range(PACK):
                    nc.scalar.activation(z_planar[:, t, :], logs[:, t, :], ACT.Copy, scale=neg_gain[:, t : t + 1])
                nc.scalar.copy(by_lines_packed(zb[:]), by_lines_planar(z_planar[:]))
            else:
                logs = keep.tile([P, width, PACK], F32, name="logs%d" % c)
                nc.scalar.activation(by_lines_packed(logs[:]), by_lines_planar(sums[c][:]), ACT.Ln)
                nc.vector.tensor_tensor(zb[:], logs[:], neg_gain[:].unsqueeze(1).to_broadcast([P, width, PACK]), ALU.mult)
            nc.vector.quantize_mx(out=zw[:, lo:hi].bitcast(FP8X4), scales=zs[:, lo:hi], in_=zb[:].rearrange("p j t -> p (j t)"))
            for t in range(PACK):
                product(h_columns(t, lo, hi), t, w2w, w2s, zw[:, lo:hi], zs[:, lo:hi])

        for t in range(PACK):
            for n, ((lo, hi), h_acc) in enumerate(zip(pieces[t], h_accs[t])):
                nc.scalar.copy(h_rows[t][:, lo:hi], h_acc[:])
                if n == 0:
                    nc.scalar.activation(h_less[t][:, lo:hi], h_acc[:], ACT.Copy, bias=-0.5)
        for t in range(PACK):
            for (lo, hi), h_acc in zip(pieces[t][1:], h_accs[t][1:]):
                nc.scalar.activation(h_less[t][:, lo:hi], h_acc[:], ACT.Copy, bias=-0.5)

        ow = keep.tile([P, S], U32, name="ow", align_bytes=64)
        osc = keep.tile([P, S], U8, name="osc", align_bytes=64)
        out_rows = out_0.rearrange("(p t) j -> p t j", t=PACK)
        out_words = words_view(out_1)
        res = [keep.tile([P, PACK, hi - lo], F32, name="res%d" % lo) for lo, hi in CHUNKS]
        d2 = [keep.tile([P, PACK, hi - lo], F32, name="d2_%d" % lo) for lo, hi in CHUNKS]
        d3 = [keep.tile([P, PACK, hi - lo], F32, name="d3_%d" % lo) for lo, hi in CHUNKS]
        last = len(CHUNKS) - 1

        def margins(c, tiles):
            lo, hi = CHUNKS[c]
            for t in tiles:
                for margin, list_tile in ((d2[c], n2_t), (d3[c], n3_t)):
                    nc.vector.tensor_tensor(
                        margin[:, t, :], h_rows[t][:].indirect(entries(list_tile, lo, hi)), h_less[t][:, lo:hi], ALU.subtract
                    )

        def hinge(c):
            nc.vector.scalar_tensor_tensor(res[c][:], d2[c][:], 0.0, d3[c][:], ALU.max, ALU.max)

        def store_and_round(c):
            lo, hi = CHUNKS[c]
            nc.sync.dma_start(out=out_rows[:, :, lo:hi], in_=res[c][:])
            ob = keep.tile([P, hi - lo, PACK], BF16, name="ob%d" % c, align_bytes=64)
            if c == last:
                nc.vector.tensor_copy(by_lines_packed(ob[:]), by_lines_planar(res[c][:]))
            else:
                nc.scalar.copy(by_lines_packed(ob[:]), by_lines_planar(res[c][:]))
            return ob

        def quantise(c, ob):
            lo, hi = CHUNKS[c]
            nc.vector.quantize_mx(out=ow[:, lo:hi].bitcast(FP8X4), scales=osc[:, lo:hi], in_=ob[:].rearrange("p j t -> p (j t)"))
            nc.sync.dma_start(out=out_words[:, lo:hi], in_=ow[:, lo:hi].bitcast(I32))

        for c in range(len(CHUNKS)):
            margins(c, range(1))
            if c > 0:
                hinge(c - 1)
                rounded = store_and_round(c - 1)
            margins(c, range(1, PACK))
            if c > 0:
                quantise(c - 1, rounded)
        hinge(last)
        quantise(last, store_and_round(last))

        for q in range(QUADRANTS):
            queue = nc.scalar if q % 2 else nc.sync
            queue.dma_start(out=out_2[0].bitcast(I32)[4 * q : 4 * q + 4, :], in_=osc[32 * q : 32 * q + 4, :].bitcast(I32))
